import numpy as np
CORES = [4,12,20,28,36,44,52,60,68,76,84,92,100,108,116,124]
N = 16
ROOT = 0
def setup_inputs(rng):
    return {"x": rng.standard_normal((N, 128, N * 2), dtype=np.float32)}
def reference(x):
    return {"y": np.stack([x[ROOT][:, r * 2:(r + 1) * 2] for r in range(N)])}

@@ -1,0 +1,50 @@
+import concourse.bass as bass
+
+SCRATCH = {
+    "xs": ("sbuf", [128, 32], "float32"),
+    "slab": ("dram", [128, 8], "float32"),
+}
+SEMAPHORES = ["loaded", "stored", "arrived", "sent"]
+
+
+def rank_program(g, core, T, topo):
+    root = T.cores[0]
+    base = topo.chip(root) * 8
+    helpers = [base + 6, base + 7, base + 2, base + 3]
+
+    def ids(dsts):
+        out = []
+        for c in dsts:
+            rid, pid, se = topo.addr(c)
+            out.append(bass.DstId(rid=rid, pnc=pid))
+        return out
+
+    if core == root:
+        g.dma_start(T.xs[:], T.x[:]).then_inc(T.sem.loaded, 16)
+        g.wait_ge(T.sem.loaded, 16)
+        g.remote_dma_fused(
+            [bass.RemoteDMATransfer(dst_ids=ids([h]), dma_engine_mask=0xF << (4 * i), remote_sem=T.sem.arrived,
+                                    srcs=[T.xs[:, 8 * i:8 * i + 8]], dsts=[T.slab[:]])
+             for i, h in enumerate(helpers)], local_sem=T.sem.sent)
+        g.dma_start(T.y[:], T.x[:, 0:2]).then_inc(T.sem.stored, 16)
+        g.wait_ge(T.sem.sent, 16)
+        g.wait_ge(T.sem.stored, 16)
+        return
+
+    if core in helpers:
+        i = helpers.index(core)
+        dsts = [c for c in T.cores[4 * i:4 * i + 4] if c != root]
+        g.wait_ge(T.sem.arrived, 4)
+        g.remote_dma_fused(
+            [bass.RemoteDMATransfer(dst_ids=ids(dsts), dma_engine_mask=0x00FF, remote_sem=T.sem.arrived,
+                                    srcs=[T.slab[:]], dsts=[T.slab[:] for c in dsts])], local_sem=T.sem.sent)
+        g.wait_ge(T.sem.sent, 8)
+        return
+
+    rank = T.rank_of(core)
+    if rank is None:
+        return
+    k = rank % 4
+    g.wait_ge(T.sem.arrived, 8)
+    g.dma_start(T.y[:], T.slab[:, 2 * k:2 * k + 2]).then_inc(T.sem.stored, 16)
+    g.wait_ge(T.sem.stored, 16)

@@ -1,8 +1,7 @@
 import concourse.bass as bass
 
 SCRATCH = {
-    "xs": ("sbuf", [128, 32], "float32"),
-    "slab": ("dram", [128, 8], "float32"),
+    "xd": ("dram", [128, 32], "float32"),
 }
 SEMAPHORES = ["loaded", "stored", "arrived", "sent"]
 
@@ -11,40 +10,37 @@ def rank_program(g, core, T, topo):
     root = T.cores[0]
     base = topo.chip(root) * 8
     helpers = [base + 6, base + 7, base + 2, base + 3]
+    far = [c for c in T.cores if (topo.chip(c) ^ topo.chip(root)) & 1]
+    near = [c for c in T.cores if c != root and not (topo.chip(c) ^ topo.chip(root)) & 1]
+    share = {h: far[2 * i:2 * i + 2] for i, h in enumerate(helpers)}
 
-    def ids(dsts):
-        out = []
+    def copy_to(dsts, mask):
+        ids = []
         for c in dsts:
             rid, pid, se = topo.addr(c)
-            out.append(bass.DstId(rid=rid, pnc=pid))
-        return out
+            ids.append(bass.DstId(rid=rid, pnc=pid))
+        return bass.RemoteDMATransfer(dst_ids=ids, dma_engine_mask=mask, remote_sem=T.sem.arrived,
+                                      srcs=[T.xd[:]], dsts=[T.xd[:] for c in dsts])
 
     if core == root:
-        g.dma_start(T.xs[:], T.x[:]).then_inc(T.sem.loaded, 16)
+        g.dma_start(T.xd[:], T.x[:]).then_inc(T.sem.loaded, 16)
         g.wait_ge(T.sem.loaded, 16)
-        g.remote_dma_fused(
-            [bass.RemoteDMATransfer(dst_ids=ids([h]), dma_engine_mask=0xF << (4 * i), remote_sem=T.sem.arrived,
-                                    srcs=[T.xs[:, 8 * i:8 * i + 8]], dsts=[T.slab[:]])
-             for i, h in enumerate(helpers)], local_sem=T.sem.sent)
+        g.remote_dma_fused([copy_to(helpers, 0xFFFF)], local_sem=T.sem.sent)
+        g.remote_dma_fused([copy_to(near, 0x00FF)], local_sem=T.sem.sent)
         g.dma_start(T.y[:], T.x[:, 0:2]).then_inc(T.sem.stored, 16)
-        g.wait_ge(T.sem.sent, 16)
+        g.wait_ge(T.sem.sent, 24)
         g.wait_ge(T.sem.stored, 16)
         return
 
-    if core in helpers:
-        i = helpers.index(core)
-        dsts = [c for c in T.cores[4 * i:4 * i + 4] if c != root]
-        g.wait_ge(T.sem.arrived, 4)
-        g.remote_dma_fused(
-            [bass.RemoteDMATransfer(dst_ids=ids(dsts), dma_engine_mask=0x00FF, remote_sem=T.sem.arrived,
-                                    srcs=[T.slab[:]], dsts=[T.slab[:] for c in dsts])], local_sem=T.sem.sent)
+    if core in share:
+        g.wait_ge(T.sem.arrived, 16)
+        g.remote_dma_fused([copy_to(share[core], 0x00FF)], local_sem=T.sem.sent)
         g.wait_ge(T.sem.sent, 8)
         return
 
     rank = T.rank_of(core)
     if rank is None:
         return
-    k = rank % 4
     g.wait_ge(T.sem.arrived, 8)
-    g.dma_start(T.y[:], T.slab[:, 2 * k:2 * k + 2]).then_inc(T.sem.stored, 16)
+    g.dma_start(T.y[:], T.xd[:, 2 * rank:2 * rank + 2]).then_inc(T.sem.stored, 16)
     g.wait_ge(T.sem.stored, 16)

@@ -9,10 +9,11 @@ SEMAPHORES = ["loaded", "stored", "arrived", "sent"]
 def rank_program(g, core, T, topo):
     root = T.cores[0]
     base = topo.chip(root) * 8
-    helpers = [base + 6, base + 7, base + 2, base + 3]
     far = [c for c in T.cores if (topo.chip(c) ^ topo.chip(root)) & 1]
     near = [c for c in T.cores if c != root and not (topo.chip(c) ^ topo.chip(root)) & 1]
-    share = {h: far[2 * i:2 * i + 2] for i, h in enumerate(helpers)}
+    share = {base + 6: far[0:2], base + 7: far[2:4], base + 2: far[4:6], base + 3: far[6:8],
+             base + 0: near[3:5], base + 1: near[5:7]}
+    direct = near[0:3]
 
     def copy_to(dsts, mask):
         ids = []
@@ -25,8 +26,8 @@ def rank_program(g, core, T, topo):
     if core == root:
         g.dma_start(T.xd[:], T.x[:]).then_inc(T.sem.loaded, 16)
         g.wait_ge(T.sem.loaded, 16)
-        g.remote_dma_fused([copy_to(helpers, 0xFFFF)], local_sem=T.sem.sent)
-        g.remote_dma_fused([copy_to(near, 0x00FF)], local_sem=T.sem.sent)
+        g.remote_dma_fused([copy_to(list(share), 0xFFFF)], local_sem=T.sem.sent)
+        g.remote_dma_fused([copy_to(direct, 0x00FF)], local_sem=T.sem.sent)
         g.dma_start(T.y[:], T.x[:, 0:2]).then_inc(T.sem.stored, 16)
         g.wait_ge(T.sem.sent, 24)
         g.wait_ge(T.sem.stored, 16)

import concourse.bass as bass

SCRATCH = {
    "xd": ("dram", [128, 32], "float32"),
}
SEMAPHORES = ["loaded", "stored", "arrived", "sent"]


def rank_program(g, core, T, topo):
    root = T.cores[0]
    base = topo.chip(root) * 8
    far = [c for c in T.cores if (topo.chip(c) ^ topo.chip(root)) & 1]
    near = [c for c in T.cores if c != root and not (topo.chip(c) ^ topo.chip(root)) & 1]
    share = {base + 6: far[0:2], base + 7: far[2:4], base + 2: far[4:6], base + 3: far[6:8],
             base + 0: near[3:5], base + 1: near[5:7]}
    direct = near[0:3]

    def copy_to(dsts, mask):
        ids = []
        for c in dsts:
            rid, pid, se = topo.addr(c)
            ids.append(bass.DstId(rid=rid, pnc=pid))
        return bass.RemoteDMATransfer(dst_ids=ids, dma_engine_mask=mask, remote_sem=T.sem.arrived,
                                      srcs=[T.xd[:]], dsts=[T.xd[:] for c in dsts])

    if core == root:
        g.dma_start(T.xd[:], T.x[:]).then_inc(T.sem.loaded, 16)
        g.wait_ge(T.sem.loaded, 16)
        g.remote_dma_fused([copy_to(list(share), 0xFFFF)], local_sem=T.sem.sent)
        g.remote_dma_fused([copy_to(direct, 0x00FF)], local_sem=T.sem.sent)
        g.dma_start(T.y[:], T.x[:, 0:2]).then_inc(T.sem.stored, 16)
        g.wait_ge(T.sem.sent, 24)
        g.wait_ge(T.sem.stored, 16)
        return

    if core in share:
        g.wait_ge(T.sem.arrived, 16)
        g.remote_dma_fused([copy_to(share[core], 0x00FF)], local_sem=T.sem.sent)
        g.wait_ge(T.sem.sent, 8)
        return

    rank = T.rank_of(core)
    if rank is None:
        return
    g.wait_ge(T.sem.arrived, 8)
    g.dma_start(T.y[:], T.xd[:, 2 * rank:2 * rank + 2]).then_inc(T.sem.stored, 16)
    g.wait_ge(T.sem.stored, 16)
